import numpy as np
import ml_dtypes


def mxq(x, axis, fmt="e4m3"):
    dtype, down = {"e4m3": (ml_dtypes.float8_e4m3fn, 7), "e5m2": (ml_dtypes.float8_e5m2, 14)}[fmt]
    v = np.moveaxis(np.asarray(x, np.float32).astype(ml_dtypes.bfloat16).astype(np.float64), axis, -1)
    blocks = v.reshape(v.shape[:-1] + (-1, 32))
    amax = np.abs(blocks).max(-1, keepdims=True)
    byte = np.maximum(np.where(amax > 0, np.frexp(amax)[1] - 1 + 127, 0) - down, 1)
    scale = np.exp2(byte - 127.0)
    codes = (blocks / scale).astype(np.float32).astype(dtype).astype(np.float64)
    return np.moveaxis((codes * scale).reshape(v.shape), -1, axis)


WIDE = False


def mx_kscale(k):
    if not WIDE:
        return np.ones(k)
    levels = np.array([10, -10, 5, -5, 0])
    if k % 512:
        return np.exp2(np.random.permutation(np.resize(levels, k // 32))).repeat(32)
    a = np.empty((k // 512, 16))
    for p in range(k // 512):
        a[p, :8] = np.random.permutation(np.resize(levels, 8))
        for g in range(8):
            far = levels[np.abs(levels - a[p, g]) >= 10]
            a[p, g + 8] = far[np.random.randint(len(far))]
    return np.exp2(a.ravel()).repeat(32)


def f64(x):
    return np.asarray(x).astype(np.float64)


def striped(idx):
    return np.tile(np.asarray(idx).reshape(-1, 16).T, (8, 1)).astype(np.uint16)


def unstriped(offs):
    return offs[:16].T.reshape(-1).astype(np.int64)


E2M1 = np.array([0.0, 0.5, 1.0, 1.5, 2.0, 3.0, 4.0, 6.0, -0.0, -0.5, -1.0, -1.5, -2.0, -3.0, -4.0, -6.0])


def pack_weight(w, fmt):
    k, n = w.shape
    w = f64(np.asarray(w, np.float32).astype(ml_dtypes.bfloat16)).reshape(k // 32, 32, n)
    amax = np.abs(w).max(1)
    if fmt == "e4m3":
        byte = np.frexp(amax)[1] - 1 + 127 - 7
    else:
        mant, ex = np.frexp(amax / 6.0)
        byte = np.where(mant > 0.5, ex, ex - 1) + 127
    byte = np.clip(np.where(amax > 0, byte, 1), 1, 254)
    scaled = (w * np.exp2(127.0 - byte)[:, None, :]).reshape(k, n).astype(np.float32)
    by_word = np.ascontiguousarray(scaled.reshape(k // 512, 128, 4, n).transpose(0, 1, 3, 2))
    if fmt == "e4m3":
        words = by_word.astype(ml_dtypes.float8_e4m3fn).view(np.uint8)
    else:
        c = by_word.astype(ml_dtypes.float4_e2m1fn).view(np.uint8) & 0xF
        words = (c[..., 0::2] | (c[..., 1::2] << 4)).reshape(k // 512, 128, 2 * n)
    return np.ascontiguousarray(words), np.ascontiguousarray(byte.astype(np.uint8).reshape(k // 512, 16, n))


def unpack_weight(words, scales, fmt):
    g, _, n = scales.shape
    words = np.ascontiguousarray(words).reshape(g, 128, n, -1)
    if fmt == "e4m3":
        vals = words.view(ml_dtypes.float8_e4m3fn).astype(np.float64)
    else:
        nib = np.empty((g, 128, n, 4), np.uint8)
        nib[..., 0::2] = words & 0xF
        nib[..., 1::2] = words >> 4
        vals = E2M1[nib]
    vals = vals * np.repeat(np.exp2(scales.astype(np.float64) - 127.0), 8, axis=1)[..., None]
    return vals.transpose(0, 1, 3, 2).reshape(g * 512, n)


def sigmoid(v):
    return 1.0 / (1.0 + np.exp(-v))


D, E, T, I, Q = 512, 512, 2048, 512, 128


def setup_inputs():
    n = np.random.standard_normal
    idx = np.random.permutation(T)[:I]
    idx2 = np.random.permutation(I)[:I]
    fd = mx_kscale(D)
    fe = mx_kscale(E)
    keysp = pack_weight(n((D, T)) / fd[:, None], "e4m3")
    valsp = pack_weight(n((E, T)) / fe[:, None], "e4m3")
    return {
        "query": (n((D, Q)) * 0.7 / np.sqrt(D) * fd[:, None]).astype(np.float32),
        "lam": (np.random.uniform(0.5, 2.0, (Q, 1))).astype(np.float32),
        "keys_words": keysp[0],
        "keys_scales": keysp[1],
        "gout": (n((E, Q)) * 1 / np.sqrt(E) * fe[:, None]).astype(np.float32),
        "vals_words": valsp[0],
        "vals_scales": valsp[1],
        "size": (np.random.uniform(0.5, 2.0, (1, I))).astype(np.float32),
        "dquery": (n((D, Q)) * 1.0 / np.sqrt(D) * fd[:, None]).astype(np.float32),
        "base": (0.5 * n((Q, I))).astype(np.float32),
        "offs": striped(idx),
        "offs2": striped(idx2),
    }


def reference(query, lam, keys_words, keys_scales, gout, vals_words, vals_scales, size, dquery, base, offs, offs2):
    idx = unstriped(offs)
    idx2 = unstriped(offs2)
    keysu = unpack_weight(keys_words, keys_scales, "e4m3")
    valsu = unpack_weight(vals_words, vals_scales, "e4m3")
    queryq = mxq(f64(query), 0, "e4m3")
    keysidxg = keysu[:, idx]
    a = queryq.T @ keysidxg
    dqueryq = mxq(f64(dquery), 0, "e4m3")
    ta = dqueryq.T @ keysidxg
    b = sigmoid(a)
    s = a + b[:, idx2] * f64(lam)
    p = np.exp(s - np.max(s, axis=1, keepdims=True))
    z = np.sum(p, axis=1, keepdims=True)
    goutq = mxq(f64(gout), 0, "e4m3")
    valsidxg = valsu[:, idx]
    c0 = goutq.T @ valsidxg
    dz = np.sum(c0 * p * f64(size) / np.square(z) * (-1.0), axis=1, keepdims=True)
    dp = c0 / z * f64(size) + dz
    ds = dp * p
    e1 = ds * f64(lam)
    s1 = np.zeros((Q, I))
    s1[:, idx2] = e1
    xb = ta * b * (1.0 - b)
    xs = ta + xb[:, idx2] * f64(lam)
    xp = xs * p
    xz = np.sum(xp, axis=1, keepdims=True)
    xdz = np.sum((xp * f64(size) * c0 - xz * z * 2.0 * c0 * p * f64(size) / np.square(z)) / np.square(z) * (-1.0), axis=1, keepdims=True)
    xdp = xz * c0 / np.square(z) * (-1.0) * f64(size) + xdz
    xds = xdp * p + xp * dp
    xe1 = xds * f64(lam)
    xs1 = np.zeros((Q, I))
    xs1[:, idx2] = xe1
    xda = xds + (xs1 * b + xb * s1) * (1.0 - b) + xb * (-1.0) * s1 * b
    y = xda * 512.0 + f64(base)
    return y

@@ -1,0 +1,227 @@
+from contextlib import ExitStack
+
+import concourse.mybir as mybir
+from concourse.masks import make_identity
+
+D, T, I, Q = 512, 2048, 512, 128
+FLOPS = 3 * 2 * D * Q * I
+
+F32 = mybir.dt.float32
+BF16 = mybir.dt.bfloat16
+I32 = mybir.dt.int32
+U32 = mybir.dt.uint32
+U16 = mybir.dt.uint16
+U8 = mybir.dt.uint8
+FP8X4 = mybir.dt.float8_e4m3fn_x4
+ALU = mybir.AluOpType
+ACT = mybir.ActivationFunctionType
+AX = mybir.AxisListType
+
+P = 128
+HALF = I // 2
+GAIN = 512.0
+VECTOR_SHARE = 160
+
+
+def tile_attend_hvlinked_kernel(tc, query, lam, keys_words, keys_scales, gout, vals_words, vals_scales,
+                                 size, dquery, base, offs, offs2, out):
+    nc = tc.nc
+    with ExitStack() as ctx:
+        sb = ctx.enter_context(tc.tile_pool(name="sb", bufs=1))
+        ps = ctx.enter_context(tc.psum_pool(name="ps", bufs=1))
+
+        def tile(name, shape, dtype=F32, after=None):
+            return sb.tile(shape, dtype, name=name, tag=after or name, align_bytes=64)
+
+        def entries(lst, cols):
+            return lst[:, cols.start // 16 : cols.stop // 16]
+
+        halves = [slice(0, HALF), slice(HALF, I)]
+
+        lst = sb.tile([P, I // 16], U16, name="lst")
+        lst2 = sb.tile([P, I // 16], U16, name="lst2")
+        k_words = tile("k_words", [P, T], I32)
+        v_words = tile("v_words", [P, T], I32)
+        k_bytes = tile("k_bytes", [P, T], U8)
+        v_bytes = tile("v_bytes", [P, T], U8)
+        raw = {n: tile("raw_" + n, [P, 4, Q]) for n in ("q", "dq", "g")}
+        lam_col = tile("lam_col", [P, 1])
+        size_cols = tile("size_cols", [P, 4])
+        base_sb = tile("base_sb", [P, I])
+
+        nc.gpsimd.memset(k_bytes[:].bitcast(I32), 0)
+        nc.vector.memset(v_bytes[:].bitcast(I32), 0)
+
+        def load_bytes(engine, plane, scales, rows):
+            for r in rows:
+                engine.dma_start(out=plane[r:P:32, :].bitcast(I32), in_=scales[0, r:16:4, :].bitcast(I32))
+
+        def load_words(words_sb, words):
+            nc.sync.dma_start(out=words_sb[:], in_=words[0].rearrange("p n t -> p (n t)").bitcast(I32))
+
+        def load_rows(name, src):
+            nc.sync.dma_start(out=raw[name][:], in_=src.rearrange("(p j) w -> p j w", j=4))
+
+        nc.sync.dma_start(lst[:], offs)
+        load_rows("q", query)
+        load_bytes(nc.sync, k_bytes, keys_scales, range(4))
+        load_words(k_words, keys_words)
+        load_bytes(nc.sync, v_bytes, vals_scales, range(4))
+        nc.sync.dma_start(lst2[:], offs2)
+        load_words(v_words, vals_words)
+        load_rows("g", gout)
+        load_rows("dq", dquery)
+        nc.sync.dma_start(out=base_sb[:], in_=base)
+        nc.gpsimd.dma_start(out=lam_col[:], in_=lam)
+        with nc.allow_non_contiguous_dma(reason="one weight a partition"):
+            nc.gpsimd.dma_start(out=size_cols[:], in_=size.rearrange("o (j p) -> p (o j)", p=P))
+
+        ident = tile("ident", [P, P])
+        make_identity(nc, ident[:])
+        xs1_v = tile("xs1_v", [P, I])
+        xs1_a = tile("xs1_a", [P, I])
+        nc.gpsimd.memset(xs1_v[:], 0.0)
+        nc.gpsimd.memset(xs1_a[:], 0.0)
+        size_gain = tile("size_gain", [P, 4])
+        nc.gpsimd.tensor_scalar(size_gain[:], size_cols[:], GAIN, 0.0, ALU.mult, ALU.add)
+
+        lam_down = tile("lam_down", [P, 1])
+        neg_lam_down = tile("neg_lam_down", [P, 1])
+        nc.gpsimd.tensor_scalar(lam_down[:], lam_col[:], 1.0 / GAIN, 0.0, ALU.mult, ALU.add)
+        nc.gpsimd.tensor_scalar(neg_lam_down[:], lam_col[:], -1.0 / GAIN, 0.0, ALU.mult, ALU.add)
+
+        codes, planes, grouped = {}, {}, {}
+
+        def interleave(name, engine):
+            grouped[name] = tile("grouped_" + name, [P, Q, 4], BF16)
+            engine.tensor_copy(out=grouped[name][:], in_=raw[name][:].rearrange("p t w -> p w t"))
+
+        def quantise(name):
+            codes[name] = tile("codes_" + name, [P, Q], U32)
+            planes[name] = tile("plane_" + name, [P, Q], U8)
+            nc.vector.quantize_mx(out=codes[name][:].bitcast(FP8X4), scales=planes[name][:],
+                                  in_=grouped[name][:].rearrange("p w t -> p (w t)"))
+
+        kg_words = tile("kg_words", [P, I], U32)
+        vg_words = tile("vg_words", [P, I], U32)
+        kg_bytes = tile("kg_bytes", [P, I], U8)
+        vg_bytes = tile("vg_bytes", [P, I], U8)
+
+        nc.vector.tensor_copy(kg_bytes[:], k_bytes[:].indirect(lst[:]))
+        interleave("q", nc.vector)
+        quantise("q")
+
+        th = tile("th", [P, I])
+        b = tile("b", [P, I])
+        a_ps = [ps.tile([P, HALF], F32, name="a_ps%d" % h) for h in range(2)]
+        for h, cols in enumerate(halves):
+            nc.vector.tensor_copy(kg_words[:, cols], k_words[:].bitcast(U32).indirect(entries(lst, cols)))
+            nc.tensor.matmul_mx(out=a_ps[h][:], lhsT=codes["q"][:].bitcast(FP8X4), lhsT_scale=planes["q"][:],
+                                rhs=kg_words[:, cols].bitcast(FP8X4), rhs_scale=kg_bytes[:, cols], start=True, stop=True)
+            nc.scalar.activation(out=th[:, cols], in_=a_ps[h][:], func=ACT.Tanh, scale=0.5)
+            nc.scalar.activation(out=b[:, cols], in_=th[:, cols], func=ACT.Copy, scale=0.5, bias=0.5)
+        nc.vector.tensor_copy(vg_bytes[:], v_bytes[:].indirect(lst[:]))
+
+        bg = tile("bg", [P, I])
+        for cols in halves:
+            nc.scalar.activation(out=bg[:, cols], in_=b[:].indirect(entries(lst2, cols)), func=ACT.Copy)
+        for cols in halves:
+            nc.vector.tensor_copy(vg_words[:, cols], v_words[:].bitcast(U32).indirect(entries(lst, cols)))
+        interleave("g", nc.gpsimd)
+        interleave("dq", nc.gpsimd)
+
+        s = tile("s", [P, I], after="v_words")
+        for h, cols in enumerate(halves):
+            nc.vector.scalar_tensor_tensor(s[:, cols], bg[:, cols], lam_col[:], a_ps[h][:], ALU.mult, ALU.add)
+        quantise("g")
+        neg_max = tile("neg_max", [P, 1], after="grouped_g")
+        nc.vector.tensor_reduce(neg_max[:], s[:], AX.X, ALU.max, negate=True)
+        quantise("dq")
+        sq = tile("sq", [P, I], after="b")
+        f = tile("f", [P, I])
+        nc.scalar.activation(out=sq[:], in_=th[:], func=ACT.Square)
+        nc.scalar.activation(out=f[:], in_=sq[:], func=ACT.Copy, scale=-0.25, bias=0.25)
+
+        ct_ps = [ps.tile([P, 2, Q], F32, name="ct_ps%d" % h) for h in range(2)]
+        ct = tile("ct", [P, 4, Q])
+        c_ps = ps.tile([P, I], F32, name="c_ps")
+        for j in range(4):
+            cols = slice(j * P, (j + 1) * P)
+            nc.tensor.matmul_mx(out=ct_ps[j // 2][:, j % 2, :], lhsT=vg_words[:, cols].bitcast(FP8X4), lhsT_scale=vg_bytes[:, cols],
+                                rhs=codes["g"][:].bitcast(FP8X4), rhs_scale=planes["g"][:], start=True, stop=True)
+        ta_ps = ps.tile([P, I], F32, name="ta_ps")
+        nc.tensor.matmul_mx(out=ta_ps[:], lhsT=codes["dq"][:].bitcast(FP8X4), lhsT_scale=planes["dq"][:],
+                            rhs=kg_words[:].bitcast(FP8X4), rhs_scale=kg_bytes[:], start=True, stop=True)
+        for j in range(2):
+            nc.scalar.activation(out=ct[:, j, :], in_=ct_ps[0][:, j, :], func=ACT.Copy, scale=size_gain[:, j : j + 1])
+        for j in range(2, 4):
+            nc.vector.tensor_scalar(ct[:, j, :], ct_ps[1][:, j - 2, :], size_gain[:, j : j + 1], None, ALU.mult)
+        for j in range(4):
+            nc.tensor.transpose(c_ps[:, j * P : (j + 1) * P], ct[:, j, :], ident[:])
+
+        p = tile("p", [P, I])
+        z = tile("z", [P, 1])
+        nc.scalar.activation(out=p[:], in_=s[:], func=ACT.Exp, bias=neg_max[:], accum_out=z[:])
+
+        xb = tile("xb", [P, I])
+        nc.vector.tensor_tensor(xb[:], f[:], ta_ps[:], ALU.mult)
+        xbg = tile("xbg", [P, I])
+        for cols in halves:
+            nc.scalar.activation(out=xbg[:, cols], in_=xb[:].indirect(entries(lst2, cols)), func=ACT.Copy)
+
+        r = tile("r", [P, 1])
+        nc.vector.reciprocal(r[:], z[:])
+        pn = tile("pn", [P, I])
+        nc.gpsimd.tensor_scalar(pn[:], p[:], r[:], 0.0, ALU.mult, ALU.add)
+
+        prod = tile("prod", [P, I])
+        m = tile("m", [P, 1])
+        nc.vector.scalar_tensor_tensor(prod[:], c_ps[:], r[:], p[:], ALU.mult, ALU.mult, accum_out=m[:])
+        d = tile("d", [P, I])
+        nc.vector.scalar_tensor_tensor(d[:], c_ps[:], m[:], pn[:], ALU.subtract, ALU.mult)
+
+        e1 = tile("e1", [P, I], after="xb")
+        s1 = tile("s1", [P, I])
+        nc.scalar.activation(out=e1[:], in_=d[:], func=ACT.Copy, scale=lam_down[:])
+        for cols in halves:
+            nc.scalar.activation(out=s1[:].indirect(entries(lst2, cols)), in_=e1[:, cols], func=ACT.Copy)
+
+        xs = tile("xs", [P, I], after="m")
+        nc.vector.scalar_tensor_tensor(xs[:], xbg[:], lam_col[:], ta_ps[:], ALU.mult, ALU.add)
+        prod2 = tile("prod2", [P, I], after="prod")
+        mu = tile("mu", [P, 1])
+        nc.vector.scalar_tensor_tensor(prod2[:], xs[:], r[:], p[:], ALU.mult, ALU.mult, accum_out=mu[:])
+        w = [tile("w0", [P, HALF], after="prod")]
+        nc.vector.tensor_tensor(w[0][:], th[:, halves[0]], ta_ps[:, halves[0]], ALU.mult)
+        u = tile("u", [P, I])
+        k = tile("k", [P, 1])
+        nc.vector.scalar_tensor_tensor(u[:], xs[:], mu[:], d[:], ALU.subtract, ALU.mult, accum_out=k[:])
+        w.append(tile("w1", [P, HALF], after="mu"))
+        nc.vector.tensor_tensor(w[1][:], th[:, halves[1]], ta_ps[:, halves[1]], ALU.mult)
+        nx = tile("nx", [P, I])
+        nc.vector.scalar_tensor_tensor(nx[:], pn[:], k[:], u[:], ALU.mult, ALU.subtract)
+        v_cols, a_cols = slice(0, VECTOR_SHARE), slice(VECTOR_SHARE, I)
+        xe1_a = tile("xe1_a", [P, I - VECTOR_SHARE])
+        xe1_v = tile("xe1_v", [P, VECTOR_SHARE])
+        nc.vector.tensor_scalar(xe1_a[:], nx[:, a_cols], neg_lam_down[:], None, ALU.mult)
+        nc.vector.tensor_scalar(xe1_v[:], nx[:, v_cols], neg_lam_down[:], None, ALU.mult)
+        nc.scalar.activation(out=xs1_a[:].indirect(entries(lst2, a_cols)), in_=xe1_a[:], func=ACT.Copy)
+        nc.vector.tensor_copy(xs1_v[:].indirect(entries(lst2, v_cols)), xe1_v[:])
+
+        y0 = tile("y0", [P, I])
+        nc.vector.tensor_tensor(y0[:], base_sb[:], nx[:], ALU.subtract)
+        t1 = tile("t1", [P, I], after="xe1_v")
+        for h, cols in enumerate(halves):
+            nc.vector.tensor_tensor(t1[:, cols], s1[:, cols], w[h][:], ALU.mult)
+        t2 = tile("t2", [P, I])
+        nc.vector.tensor_tensor(t2[:], xs1_v[:], t1[:], ALU.subtract)
+        t3 = tile("t3", [P, I])
+        t4 = tile("t4", [P, I])
+        y = tile("y", [P, I])
+        for cols in halves:
+            nc.vector.tensor_tensor(t3[:, cols], t2[:, cols], xs1_a[:, cols], ALU.add)
+        for cols in halves:
+            nc.vector.scalar_tensor_tensor(t4[:, cols], t3[:, cols], GAIN, f[:, cols], ALU.mult, ALU.mult)
+        for cols in halves:
+            nc.vector.tensor_tensor(y[:, cols], t4[:, cols], y0[:, cols], ALU.add)
+            nc.sync.dma_start(out=out[:, cols], in_=y[:, cols])

@@ -21,6 +21,7 @@ P = 128
 HALF = I // 2
 GAIN = 512.0
 VECTOR_SHARE = 160
+LOOKUP_SHARE = 0
 
 
 def tile_attend_hvlinked_kernel(tc, query, lam, keys_words, keys_scales, gout, vals_words, vals_scales,
@@ -29,32 +30,36 @@ def tile_attend_hvlinked_kernel(tc, query, lam, keys_words, keys_scales, gout, v
     with ExitStack() as ctx:
         sb = ctx.enter_context(tc.tile_pool(name="sb", bufs=1))
         ps = ctx.enter_context(tc.psum_pool(name="ps", bufs=1))
+        shared = ctx.enter_context(tc.tile_pool(name="shared", bufs=1))
 
         def tile(name, shape, dtype=F32, after=None):
+            if isinstance(after, int):
+                return shared.tile(shape, dtype, name=name, offset=after, align_bytes=64)
             return sb.tile(shape, dtype, name=name, tag=after or name, align_bytes=64)
 
         def entries(lst, cols):
             return lst[:, cols.start // 16 : cols.stop // 16]
 
         halves = [slice(0, HALF), slice(HALF, I)]
+        ends = [slice(0, 256), slice(256, I)]
 
         lst = sb.tile([P, I // 16], U16, name="lst")
         lst2 = sb.tile([P, I // 16], U16, name="lst2")
         k_words = tile("k_words", [P, T], I32)
-        v_words = tile("v_words", [P, T], I32)
+        v_words = tile("v_words", [P, T], I32, after=0)
         k_bytes = tile("k_bytes", [P, T], U8)
-        v_bytes = tile("v_bytes", [P, T], U8)
-        raw = {n: tile("raw_" + n, [P, 4, Q]) for n in ("q", "dq", "g")}
-        lam_col = tile("lam_col", [P, 1])
+        v_bytes = tile("v_bytes", [P, T], U8, after=8192)
+        raw = {n: tile("raw_" + n, [P, 4, Q]) for n in ("q", "g", "dq")}
+        lam_tile = tile("lam_tile", [P, 1])
         size_cols = tile("size_cols", [P, 4])
         base_sb = tile("base_sb", [P, I])
 
         nc.gpsimd.memset(k_bytes[:].bitcast(I32), 0)
         nc.vector.memset(v_bytes[:].bitcast(I32), 0)
 
-        def load_bytes(engine, plane, scales, rows):
-            for r in rows:
-                engine.dma_start(out=plane[r:P:32, :].bitcast(I32), in_=scales[0, r:16:4, :].bitcast(I32))
+        def load_bytes(plane, scales, first):
+            for r in range(4):
+                nc.sync.dma_start(out=plane[first + r : P : 32, :].bitcast(I32), in_=scales[0, r:16:4, :].bitcast(I32))
 
         def load_words(words_sb, words):
             nc.sync.dma_start(out=words_sb[:], in_=words[0].rearrange("p n t -> p (n t)").bitcast(I32))
@@ -64,40 +69,33 @@ def tile_attend_hvlinked_kernel(tc, query, lam, keys_words, keys_scales, gout, v
 
         nc.sync.dma_start(lst[:], offs)
         load_rows("q", query)
-        load_bytes(nc.sync, k_bytes, keys_scales, range(4))
-        load_words(k_words, keys_words)
-        load_bytes(nc.sync, v_bytes, vals_scales, range(4))
+        load_bytes(k_bytes, keys_scales, 0)
         nc.sync.dma_start(lst2[:], offs2)
-        load_words(v_words, vals_words)
+        load_words(k_words, keys_words)
         load_rows("g", gout)
         load_rows("dq", dquery)
+        load_bytes(v_bytes, vals_scales, 4)
+        load_words(v_words, vals_words)
         nc.sync.dma_start(out=base_sb[:], in_=base)
-        nc.gpsimd.dma_start(out=lam_col[:], in_=lam)
+        nc.gpsimd.dma_start(out=lam_tile[:], in_=lam)
         with nc.allow_non_contiguous_dma(reason="one weight a partition"):
             nc.gpsimd.dma_start(out=size_cols[:], in_=size.rearrange("o (j p) -> p (o j)", p=P))
-
-        ident = tile("ident", [P, P])
-        make_identity(nc, ident[:])
         xs1_v = tile("xs1_v", [P, I])
         xs1_a = tile("xs1_a", [P, I])
         nc.gpsimd.memset(xs1_v[:], 0.0)
         nc.gpsimd.memset(xs1_a[:], 0.0)
-        size_gain = tile("size_gain", [P, 4])
-        nc.gpsimd.tensor_scalar(size_gain[:], size_cols[:], GAIN, 0.0, ALU.mult, ALU.add)
-
-        lam_down = tile("lam_down", [P, 1])
-        neg_lam_down = tile("neg_lam_down", [P, 1])
-        nc.gpsimd.tensor_scalar(lam_down[:], lam_col[:], 1.0 / GAIN, 0.0, ALU.mult, ALU.add)
-        nc.gpsimd.tensor_scalar(neg_lam_down[:], lam_col[:], -1.0 / GAIN, 0.0, ALU.mult, ALU.add)
-
         codes, planes, grouped = {}, {}, {}
 
-        def interleave(name, engine):
-            grouped[name] = tile("grouped_" + name, [P, Q, 4], BF16)
-            engine.tensor_copy(out=grouped[name][:], in_=raw[name][:].rearrange("p t w -> p w t"))
+        def interleave(name, engine, after=None):
+            grouped[name] = tile("grouped_" + name, [P, Q, 4], BF16, after)
+            if engine is nc.scalar:
+                nc.scalar.activation(out=grouped[name][:].rearrange("p (c i) t -> p c t i", i=4),
+                                     in_=raw[name][:].rearrange("p t (c i) -> p c t i", i=4), func=ACT.Copy)
+            else:
+                engine.tensor_copy(out=grouped[name][:], in_=raw[name][:].rearrange("p t w -> p w t"))
 
-        def quantise(name):
-            codes[name] = tile("codes_" + name, [P, Q], U32)
+        def quantise(name, after=None):
+            codes[name] = tile("codes_" + name, [P, Q], U32, after)
             planes[name] = tile("plane_" + name, [P, Q], U8)
             nc.vector.quantize_mx(out=codes[name][:].bitcast(FP8X4), scales=planes[name][:],
                                   in_=grouped[name][:].rearrange("p w t -> p (w t)"))
@@ -106,122 +104,121 @@ def tile_attend_hvlinked_kernel(tc, query, lam, keys_words, keys_scales, gout, v
         vg_words = tile("vg_words", [P, I], U32)
         kg_bytes = tile("kg_bytes", [P, I], U8)
         vg_bytes = tile("vg_bytes", [P, I], U8)
-
+        ct_ps = [ps.tile([P, 2, Q], F32, name="ct_ps%d" % h) for h in range(2)]
+        c_ps = ps.tile([P, I], F32, name="c_ps")
+        ta_ps = ps.tile([P, I], F32, name="ta_ps")
+        v_cols, a_cols = slice(0, VECTOR_SHARE), slice(VECTOR_SHARE, I)
         nc.vector.tensor_copy(kg_bytes[:], k_bytes[:].indirect(lst[:]))
-        interleave("q", nc.vector)
+        interleave("q", nc.scalar)
         quantise("q")
+        ident = tile("ident", [P, P])
+        make_identity(nc, ident[:])
+        factors = size_cols
+        lam_col = lam_tile[:]
+        interleave("g", nc.scalar)
+        interleave("dq", nc.scalar)
+        th = tile("th", [P, I], after="raw_dq")
 
-        th = tile("th", [P, I])
-        b = tile("b", [P, I])
-        a_ps = [ps.tile([P, HALF], F32, name="a_ps%d" % h) for h in range(2)]
-        for h, cols in enumerate(halves):
+        parts = [slice(0, 256), slice(256, I)]
+        a_ps = [ps.tile([P, cols.stop - cols.start], F32, name="a_ps%d" % h) for h, cols in enumerate(parts)]
+        for h, cols in enumerate(parts):
             nc.vector.tensor_copy(kg_words[:, cols], k_words[:].bitcast(U32).indirect(entries(lst, cols)))
             nc.tensor.matmul_mx(out=a_ps[h][:], lhsT=codes["q"][:].bitcast(FP8X4), lhsT_scale=planes["q"][:],
                                 rhs=kg_words[:, cols].bitcast(FP8X4), rhs_scale=kg_bytes[:, cols], start=True, stop=True)
             nc.scalar.activation(out=th[:, cols], in_=a_ps[h][:], func=ACT.Tanh, scale=0.5)
-            nc.scalar.activation(out=b[:, cols], in_=th[:, cols], func=ACT.Copy, scale=0.5, bias=0.5)
-        nc.vector.tensor_copy(vg_bytes[:], v_bytes[:].indirect(lst[:]))
 
-        bg = tile("bg", [P, I])
+        quantise("g")
+        nc.vector.tensor_copy(vg_bytes[:], v_bytes[:].indirect(lst[:]))
+        b = tile("b", [P, I], after=9216)
+        nc.vector.tensor_scalar(b[:], th[:], 0.5, 0.5, ALU.mult, ALU.add)
+        quantise("dq", after=8192)
+        nc.tensor.matmul_mx(out=ta_ps[:], lhsT=codes["dq"][:].bitcast(FP8X4), lhsT_scale=planes["dq"][:],
+                            rhs=kg_words[:].bitcast(FP8X4), rhs_scale=kg_bytes[:], start=True, stop=True)
+        sq = tile("sq", [P, I])
+        nc.scalar.activation(out=sq[:], in_=th[:], func=ACT.Square)
+        f = tile("f", [P, I])
+        nc.gpsimd.tensor_scalar(f[:], sq[:], -0.25, 0.25, ALU.mult, ALU.add)
+        bg = tile("bg", [P, I], after=12288)
         for cols in halves:
             nc.scalar.activation(out=bg[:, cols], in_=b[:].indirect(entries(lst2, cols)), func=ACT.Copy)
         for cols in halves:
             nc.vector.tensor_copy(vg_words[:, cols], v_words[:].bitcast(U32).indirect(entries(lst, cols)))
-        interleave("g", nc.gpsimd)
-        interleave("dq", nc.gpsimd)
-
-        s = tile("s", [P, I], after="v_words")
-        for h, cols in enumerate(halves):
-            nc.vector.scalar_tensor_tensor(s[:, cols], bg[:, cols], lam_col[:], a_ps[h][:], ALU.mult, ALU.add)
-        quantise("g")
-        neg_max = tile("neg_max", [P, 1], after="grouped_g")
-        nc.vector.tensor_reduce(neg_max[:], s[:], AX.X, ALU.max, negate=True)
-        quantise("dq")
-        sq = tile("sq", [P, I], after="b")
-        f = tile("f", [P, I])
-        nc.scalar.activation(out=sq[:], in_=th[:], func=ACT.Square)
-        nc.scalar.activation(out=f[:], in_=sq[:], func=ACT.Copy, scale=-0.25, bias=0.25)
-
-        ct_ps = [ps.tile([P, 2, Q], F32, name="ct_ps%d" % h) for h in range(2)]
-        ct = tile("ct", [P, 4, Q])
-        c_ps = ps.tile([P, I], F32, name="c_ps")
         for j in range(4):
             cols = slice(j * P, (j + 1) * P)
-            nc.tensor.matmul_mx(out=ct_ps[j // 2][:, j % 2, :], lhsT=vg_words[:, cols].bitcast(FP8X4), lhsT_scale=vg_bytes[:, cols],
+            nc.tensor.matmul_mx(out=ct_ps[j // 2][:, j % 2, :], lhsT=vg_words[:, cols].bitcast(FP8X4), lhsT_scale=vg_bytes[4:P, cols],
                                 rhs=codes["g"][:].bitcast(FP8X4), rhs_scale=planes["g"][:], start=True, stop=True)
-        ta_ps = ps.tile([P, I], F32, name="ta_ps")
-        nc.tensor.matmul_mx(out=ta_ps[:], lhsT=codes["dq"][:].bitcast(FP8X4), lhsT_scale=planes["dq"][:],
-                            rhs=kg_words[:].bitcast(FP8X4), rhs_scale=kg_bytes[:], start=True, stop=True)
+        s = tile("s", [P, I], after=0)
+        nc.vector.scalar_tensor_tensor(s[:, 0:256], bg[:, 0:256], lam_col, a_ps[0][:, 0:256], ALU.mult, ALU.add)
+        nc.vector.scalar_tensor_tensor(s[:, 256:512], bg[:, 256:512], lam_col, a_ps[1][:, 0:256], ALU.mult, ALU.add)
+        ct = tile("ct", [P, 4, Q])
         for j in range(2):
-            nc.scalar.activation(out=ct[:, j, :], in_=ct_ps[0][:, j, :], func=ACT.Copy, scale=size_gain[:, j : j + 1])
-        for j in range(2, 4):
-            nc.vector.tensor_scalar(ct[:, j, :], ct_ps[1][:, j - 2, :], size_gain[:, j : j + 1], None, ALU.mult)
-        for j in range(4):
+            nc.scalar.activation(out=ct[:, j, :], in_=ct_ps[0][:, j, :], func=ACT.Copy, scale=factors[:, j : j + 1])
             nc.tensor.transpose(c_ps[:, j * P : (j + 1) * P], ct[:, j, :], ident[:])
-
+        for j in range(2, 4):
+            nc.scalar.activation(out=ct[:, j, :], in_=ct_ps[1][:, j - 2, :], func=ACT.Copy, scale=factors[:, j : j + 1])
+            nc.tensor.transpose(c_ps[:, j * P : (j + 1) * P], ct[:, j, :], ident[:])
+        neg_max = tile("neg_max", [P, 1])
+        nc.vector.tensor_reduce(neg_max[:], s[:], AX.X, ALU.max, negate=True)
         p = tile("p", [P, I])
         z = tile("z", [P, 1])
         nc.scalar.activation(out=p[:], in_=s[:], func=ACT.Exp, bias=neg_max[:], accum_out=z[:])
-
-        xb = tile("xb", [P, I])
+        xb = tile("xb", [P, I], after=13312)
         nc.vector.tensor_tensor(xb[:], f[:], ta_ps[:], ALU.mult)
         xbg = tile("xbg", [P, I])
         for cols in halves:
             nc.scalar.activation(out=xbg[:, cols], in_=xb[:].indirect(entries(lst2, cols)), func=ACT.Copy)
-
+        w = [tile("w0", [P, HALF], after=12288)]
+        nc.vector.tensor_tensor(w[0][:], th[:, halves[0]], ta_ps[:, halves[0]], ALU.mult)
         r = tile("r", [P, 1])
         nc.vector.reciprocal(r[:], z[:])
         pn = tile("pn", [P, I])
         nc.gpsimd.tensor_scalar(pn[:], p[:], r[:], 0.0, ALU.mult, ALU.add)
-
         prod = tile("prod", [P, I])
         m = tile("m", [P, 1])
         nc.vector.scalar_tensor_tensor(prod[:], c_ps[:], r[:], p[:], ALU.mult, ALU.mult, accum_out=m[:])
+        w.append(tile("w1", [P, HALF], after="z"))
+        nc.vector.tensor_tensor(w[1][:], th[:, halves[1]], ta_ps[:, halves[1]], ALU.mult)
         d = tile("d", [P, I])
-        nc.vector.scalar_tensor_tensor(d[:], c_ps[:], m[:], pn[:], ALU.subtract, ALU.mult)
-
-        e1 = tile("e1", [P, I], after="xb")
+        for cols in halves:
+            nc.vector.scalar_tensor_tensor(d[:, cols], c_ps[:, cols], m[:], pn[:, cols], ALU.subtract, ALU.mult)
+        e1 = tile("e1", [P, I])
         s1 = tile("s1", [P, I])
-        nc.scalar.activation(out=e1[:], in_=d[:], func=ACT.Copy, scale=lam_down[:])
+        for cols in halves:
+            nc.scalar.activation(out=e1[:, cols], in_=d[:, cols], func=ACT.Copy, scale=lam_col)
         for cols in halves:
             nc.scalar.activation(out=s1[:].indirect(entries(lst2, cols)), in_=e1[:, cols], func=ACT.Copy)
-
-        xs = tile("xs", [P, I], after="m")
-        nc.vector.scalar_tensor_tensor(xs[:], xbg[:], lam_col[:], ta_ps[:], ALU.mult, ALU.add)
-        prod2 = tile("prod2", [P, I], after="prod")
+        xs = tile("xs", [P, I], after="raw_dq")
+        nc.vector.scalar_tensor_tensor(xs[:], xbg[:], lam_col, ta_ps[:], ALU.mult, ALU.add)
+        prod2 = tile("prod2", [P, I])
         mu = tile("mu", [P, 1])
         nc.vector.scalar_tensor_tensor(prod2[:], xs[:], r[:], p[:], ALU.mult, ALU.mult, accum_out=mu[:])
-        w = [tile("w0", [P, HALF], after="prod")]
-        nc.vector.tensor_tensor(w[0][:], th[:, halves[0]], ta_ps[:, halves[0]], ALU.mult)
         u = tile("u", [P, I])
         k = tile("k", [P, 1])
         nc.vector.scalar_tensor_tensor(u[:], xs[:], mu[:], d[:], ALU.subtract, ALU.mult, accum_out=k[:])
-        w.append(tile("w1", [P, HALF], after="mu"))
-        nc.vector.tensor_tensor(w[1][:], th[:, halves[1]], ta_ps[:, halves[1]], ALU.mult)
         nx = tile("nx", [P, I])
-        nc.vector.scalar_tensor_tensor(nx[:], pn[:], k[:], u[:], ALU.mult, ALU.subtract)
-        v_cols, a_cols = slice(0, VECTOR_SHARE), slice(VECTOR_SHARE, I)
         xe1_a = tile("xe1_a", [P, I - VECTOR_SHARE])
         xe1_v = tile("xe1_v", [P, VECTOR_SHARE])
-        nc.vector.tensor_scalar(xe1_a[:], nx[:, a_cols], neg_lam_down[:], None, ALU.mult)
-        nc.vector.tensor_scalar(xe1_v[:], nx[:, v_cols], neg_lam_down[:], None, ALU.mult)
+        for cols in (a_cols, v_cols):
+            nc.vector.scalar_tensor_tensor(nx[:, cols], pn[:, cols], k[:], u[:, cols], ALU.mult, ALU.subtract)
+        nc.vector.tensor_scalar(xe1_a[:], nx[:, a_cols], lam_col, -1.0, ALU.mult, ALU.mult)
+        nc.vector.tensor_scalar(xe1_v[:], nx[:, v_cols], lam_col, -1.0, ALU.mult, ALU.mult)
         nc.scalar.activation(out=xs1_a[:].indirect(entries(lst2, a_cols)), in_=xe1_a[:], func=ACT.Copy)
         nc.vector.tensor_copy(xs1_v[:].indirect(entries(lst2, v_cols)), xe1_v[:])
-
         y0 = tile("y0", [P, I])
-        nc.vector.tensor_tensor(y0[:], base_sb[:], nx[:], ALU.subtract)
+        nc.vector.scalar_tensor_tensor(y0[:], nx[:], -GAIN, base_sb[:], ALU.mult, ALU.add)
         t1 = tile("t1", [P, I], after="xe1_v")
-        for h, cols in enumerate(halves):
-            nc.vector.tensor_tensor(t1[:, cols], s1[:, cols], w[h][:], ALU.mult)
+        nc.vector.tensor_tensor(t1[:, halves[0]], s1[:, halves[0]], w[0][:], ALU.mult)
+        nc.vector.tensor_tensor(t1[:, halves[1]], s1[:, halves[1]], w[1][:], ALU.mult)
         t2 = tile("t2", [P, I])
-        nc.vector.tensor_tensor(t2[:], xs1_v[:], t1[:], ALU.subtract)
+        for cols in halves:
+            nc.vector.tensor_tensor(t2[:, cols], xs1_v[:, cols], t1[:, cols], ALU.subtract)
         t3 = tile("t3", [P, I])
         t4 = tile("t4", [P, I])
         y = tile("y", [P, I])
-        for cols in halves:
+        for cols in ends:
             nc.vector.tensor_tensor(t3[:, cols], t2[:, cols], xs1_a[:, cols], ALU.add)
-        for cols in halves:
+        for cols in ends:
             nc.vector.scalar_tensor_tensor(t4[:, cols], t3[:, cols], GAIN, f[:, cols], ALU.mult, ALU.mult)
-        for cols in halves:
+        for cols in ends:
             nc.vector.tensor_tensor(y[:, cols], t4[:, cols], y0[:, cols], ALU.add)
             nc.sync.dma_start(out=out[:, cols], in_=y[:, cols])

@@ -20,7 +20,7 @@ AX = mybir.AxisListType
 P = 128
 HALF = I // 2
 GAIN = 512.0
-VECTOR_SHARE = 160
+VECTOR_SHARE = 192
 LOOKUP_SHARE = 0
 
 
@@ -51,7 +51,7 @@ def tile_attend_hvlinked_kernel(tc, query, lam, keys_words, keys_scales, gout, v
         v_bytes = tile("v_bytes", [P, T], U8, after=8192)
         raw = {n: tile("raw_" + n, [P, 4, Q]) for n in ("q", "g", "dq")}
         lam_tile = tile("lam_tile", [P, 1])
-        size_cols = tile("size_cols", [P, 4])
+        size_rows = tile("size_rows", [P, P])
         base_sb = tile("base_sb", [P, I])
 
         nc.gpsimd.memset(k_bytes[:].bitcast(I32), 0)
@@ -78,8 +78,8 @@ def tile_attend_hvlinked_kernel(tc, query, lam, keys_words, keys_scales, gout, v
         load_words(v_words, vals_words)
         nc.sync.dma_start(out=base_sb[:], in_=base)
         nc.gpsimd.dma_start(out=lam_tile[:], in_=lam)
-        with nc.allow_non_contiguous_dma(reason="one weight a partition"):
-            nc.gpsimd.dma_start(out=size_cols[:], in_=size.rearrange("o (j p) -> p (o j)", p=P))
+        nc.gpsimd.memset(size_rows[:], 0.0)
+        nc.gpsimd.dma_start(out=size_rows[0:4, :], in_=size.rearrange("o (j p) -> (o j) p", p=P))
         xs1_v = tile("xs1_v", [P, I])
         xs1_a = tile("xs1_a", [P, I])
         nc.gpsimd.memset(xs1_v[:], 0.0)
@@ -111,10 +111,10 @@ def tile_attend_hvlinked_kernel(tc, query, lam, keys_words, keys_scales, gout, v
         nc.vector.tensor_copy(kg_bytes[:], k_bytes[:].indirect(lst[:]))
         interleave("q", nc.scalar)
         quantise("q")
-        ident = tile("ident", [P, P])
-        make_identity(nc, ident[:])
-        factors = size_cols
         lam_col = lam_tile[:]
+        neg_lam_wide = tile("neg_lam_wide", [P, VECTOR_SHARE])
+        nc.gpsimd.memset(neg_lam_wide[:], -1.0)
+        nc.gpsimd.tensor_scalar(neg_lam_wide[:], neg_lam_wide[:], lam_col, 0.0, ALU.mult, ALU.add)
         interleave("g", nc.scalar)
         interleave("dq", nc.scalar)
         th = tile("th", [P, I], after="raw_dq")
@@ -127,6 +127,10 @@ def tile_attend_hvlinked_kernel(tc, query, lam, keys_words, keys_scales, gout, v
                                 rhs=kg_words[:, cols].bitcast(FP8X4), rhs_scale=kg_bytes[:, cols], start=True, stop=True)
             nc.scalar.activation(out=th[:, cols], in_=a_ps[h][:], func=ACT.Tanh, scale=0.5)
 
+        ident = tile("ident", [P, P], after="k_words")
+        make_identity(nc, ident[:])
+        cols_ps = ps.tile([P, P], F32, name="cols_ps")
+        nc.tensor.transpose(cols_ps[:], size_rows[:], ident[:])
         quantise("g")
         nc.vector.tensor_copy(vg_bytes[:], v_bytes[:].indirect(lst[:]))
         b = tile("b", [P, I], after=9216)
@@ -141,6 +145,8 @@ def tile_attend_hvlinked_kernel(tc, query, lam, keys_words, keys_scales, gout, v
         bg = tile("bg", [P, I], after=12288)
         for cols in halves:
             nc.scalar.activation(out=bg[:, cols], in_=b[:].indirect(entries(lst2, cols)), func=ACT.Copy)
+        factors = tile("factors", [P, 4], after=9216)
+        nc.scalar.activation(out=factors[:], in_=cols_ps[:, 0:4], func=ACT.Copy)
         for cols in halves:
             nc.vector.tensor_copy(vg_words[:, cols], v_words[:].bitcast(U32).indirect(entries(lst, cols)))
         for j in range(4):
@@ -197,16 +203,14 @@ def tile_attend_hvlinked_kernel(tc, query, lam, keys_words, keys_scales, gout, v
         nc.vector.scalar_tensor_tensor(u[:], xs[:], mu[:], d[:], ALU.subtract, ALU.mult, accum_out=k[:])
         nx = tile("nx", [P, I])
         xe1_a = tile("xe1_a", [P, I - VECTOR_SHARE])
-        xe1_v = tile("xe1_v", [P, VECTOR_SHARE])
         for cols in (a_cols, v_cols):
             nc.vector.scalar_tensor_tensor(nx[:, cols], pn[:, cols], k[:], u[:, cols], ALU.mult, ALU.subtract)
         nc.vector.tensor_scalar(xe1_a[:], nx[:, a_cols], lam_col, -1.0, ALU.mult, ALU.mult)
-        nc.vector.tensor_scalar(xe1_v[:], nx[:, v_cols], lam_col, -1.0, ALU.mult, ALU.mult)
         nc.scalar.activation(out=xs1_a[:].indirect(entries(lst2, a_cols)), in_=xe1_a[:], func=ACT.Copy)
-        nc.vector.tensor_copy(xs1_v[:].indirect(entries(lst2, v_cols)), xe1_v[:])
+        nc.vector.tensor_tensor(xs1_v[:].indirect(entries(lst2, v_cols)), nx[:, v_cols], neg_lam_wide[:], ALU.mult)
         y0 = tile("y0", [P, I])
         nc.vector.scalar_tensor_tensor(y0[:], nx[:], -GAIN, base_sb[:], ALU.mult, ALU.add)
-        t1 = tile("t1", [P, I], after="xe1_v")
+        t1 = tile("t1", [P, I], after="neg_lam_wide")
         nc.vector.tensor_tensor(t1[:, halves[0]], s1[:, halves[0]], w[0][:], ALU.mult)
         nc.vector.tensor_tensor(t1[:, halves[1]], s1[:, halves[1]], w[1][:], ALU.mult)
         t2 = tile("t2", [P, I])

from contextlib import ExitStack

import concourse.mybir as mybir
from concourse.masks import make_identity

D, T, I, Q = 512, 2048, 512, 128
FLOPS = 3 * 2 * D * Q * I

F32 = mybir.dt.float32
BF16 = mybir.dt.bfloat16
I32 = mybir.dt.int32
U32 = mybir.dt.uint32
U16 = mybir.dt.uint16
U8 = mybir.dt.uint8
FP8X4 = mybir.dt.float8_e4m3fn_x4
ALU = mybir.AluOpType
ACT = mybir.ActivationFunctionType
AX = mybir.AxisListType

P = 128
HALF = I // 2
GAIN = 512.0
VECTOR_SHARE = 192
LOOKUP_SHARE = 0


def tile_attend_hvlinked_kernel(tc, query, lam, keys_words, keys_scales, gout, vals_words, vals_scales,
                                 size, dquery, base, offs, offs2, out):
    nc = tc.nc
    with ExitStack() as ctx:
        sb = ctx.enter_context(tc.tile_pool(name="sb", bufs=1))
        ps = ctx.enter_context(tc.psum_pool(name="ps", bufs=1))
        shared = ctx.enter_context(tc.tile_pool(name="shared", bufs=1))

        def tile(name, shape, dtype=F32, after=None):
            if isinstance(after, int):
                return shared.tile(shape, dtype, name=name, offset=after, align_bytes=64)
            return sb.tile(shape, dtype, name=name, tag=after or name, align_bytes=64)

        def entries(lst, cols):
            return lst[:, cols.start // 16 : cols.stop // 16]

        halves = [slice(0, HALF), slice(HALF, I)]
        ends = [slice(0, 256), slice(256, I)]

        lst = sb.tile([P, I // 16], U16, name="lst")
        lst2 = sb.tile([P, I // 16], U16, name="lst2")
        k_words = tile("k_words", [P, T], I32)
        v_words = tile("v_words", [P, T], I32, after=0)
        k_bytes = tile("k_bytes", [P, T], U8)
        v_bytes = tile("v_bytes", [P, T], U8, after=8192)
        raw = {n: tile("raw_" + n, [P, 4, Q]) for n in ("q", "g", "dq")}
        lam_tile = tile("lam_tile", [P, 1])
        size_rows = tile("size_rows", [P, P])
        base_sb = tile("base_sb", [P, I])

        nc.gpsimd.memset(k_bytes[:].bitcast(I32), 0)
        nc.vector.memset(v_bytes[:].bitcast(I32), 0)

        def load_bytes(plane, scales, first):
            for r in range(4):
                nc.sync.dma_start(out=plane[first + r : P : 32, :].bitcast(I32), in_=scales[0, r:16:4, :].bitcast(I32))

        def load_words(words_sb, words):
            nc.sync.dma_start(out=words_sb[:], in_=words[0].rearrange("p n t -> p (n t)").bitcast(I32))

        def load_rows(name, src):
            nc.sync.dma_start(out=raw[name][:], in_=src.rearrange("(p j) w -> p j w", j=4))

        nc.sync.dma_start(lst[:], offs)
        load_rows("q", query)
        load_bytes(k_bytes, keys_scales, 0)
        nc.sync.dma_start(lst2[:], offs2)
        load_words(k_words, keys_words)
        load_rows("g", gout)
        load_rows("dq", dquery)
        load_bytes(v_bytes, vals_scales, 4)
        load_words(v_words, vals_words)
        nc.sync.dma_start(out=base_sb[:], in_=base)
        nc.gpsimd.dma_start(out=lam_tile[:], in_=lam)
        nc.gpsimd.memset(size_rows[:], 0.0)
        nc.gpsimd.dma_start(out=size_rows[0:4, :], in_=size.rearrange("o (j p) -> (o j) p", p=P))
        xs1_v = tile("xs1_v", [P, I])
        xs1_a = tile("xs1_a", [P, I])
        nc.gpsimd.memset(xs1_v[:], 0.0)
        nc.gpsimd.memset(xs1_a[:], 0.0)
        codes, planes, grouped = {}, {}, {}

        def interleave(name, engine, after=None):
            grouped[name] = tile("grouped_" + name, [P, Q, 4], BF16, after)
            if engine is nc.scalar:
                nc.scalar.activation(out=grouped[name][:].rearrange("p (c i) t -> p c t i", i=4),
                                     in_=raw[name][:].rearrange("p t (c i) -> p c t i", i=4), func=ACT.Copy)
            else:
                engine.tensor_copy(out=grouped[name][:], in_=raw[name][:].rearrange("p t w -> p w t"))

        def quantise(name, after=None):
            codes[name] = tile("codes_" + name, [P, Q], U32, after)
            planes[name] = tile("plane_" + name, [P, Q], U8)
            nc.vector.quantize_mx(out=codes[name][:].bitcast(FP8X4), scales=planes[name][:],
                                  in_=grouped[name][:].rearrange("p w t -> p (w t)"))

        kg_words = tile("kg_words", [P, I], U32)
        vg_words = tile("vg_words", [P, I], U32)
        kg_bytes = tile("kg_bytes", [P, I], U8)
        vg_bytes = tile("vg_bytes", [P, I], U8)
        ct_ps = [ps.tile([P, 2, Q], F32, name="ct_ps%d" % h) for h in range(2)]
        c_ps = ps.tile([P, I], F32, name="c_ps")
        ta_ps = ps.tile([P, I], F32, name="ta_ps")
        v_cols, a_cols = slice(0, VECTOR_SHARE), slice(VECTOR_SHARE, I)
        nc.vector.tensor_copy(kg_bytes[:], k_bytes[:].indirect(lst[:]))
        interleave("q", nc.scalar)
        quantise("q")
        lam_col = lam_tile[:]
        neg_lam_wide = tile("neg_lam_wide", [P, VECTOR_SHARE])
        nc.gpsimd.memset(neg_lam_wide[:], -1.0)
        nc.gpsimd.tensor_scalar(neg_lam_wide[:], neg_lam_wide[:], lam_col, 0.0, ALU.mult, ALU.add)
        interleave("g", nc.scalar)
        interleave("dq", nc.scalar)
        th = tile("th", [P, I], after="raw_dq")

        parts = [slice(0, 256), slice(256, I)]
        a_ps = [ps.tile([P, cols.stop - cols.start], F32, name="a_ps%d" % h) for h, cols in enumerate(parts)]
        for h, cols in enumerate(parts):
            nc.vector.tensor_copy(kg_words[:, cols], k_words[:].bitcast(U32).indirect(entries(lst, cols)))
            nc.tensor.matmul_mx(out=a_ps[h][:], lhsT=codes["q"][:].bitcast(FP8X4), lhsT_scale=planes["q"][:],
                                rhs=kg_words[:, cols].bitcast(FP8X4), rhs_scale=kg_bytes[:, cols], start=True, stop=True)
            nc.scalar.activation(out=th[:, cols], in_=a_ps[h][:], func=ACT.Tanh, scale=0.5)

        ident = tile("ident", [P, P], after="k_words")
        make_identity(nc, ident[:])
        cols_ps = ps.tile([P, P], F32, name="cols_ps")
        nc.tensor.transpose(cols_ps[:], size_rows[:], ident[:])
        quantise("g")
        nc.vector.tensor_copy(vg_bytes[:], v_bytes[:].indirect(lst[:]))
        b = tile("b", [P, I], after=9216)
        nc.vector.tensor_scalar(b[:], th[:], 0.5, 0.5, ALU.mult, ALU.add)
        quantise("dq", after=8192)
        nc.tensor.matmul_mx(out=ta_ps[:], lhsT=codes["dq"][:].bitcast(FP8X4), lhsT_scale=planes["dq"][:],
                            rhs=kg_words[:].bitcast(FP8X4), rhs_scale=kg_bytes[:], start=True, stop=True)
        sq = tile("sq", [P, I])
        nc.scalar.activation(out=sq[:], in_=th[:], func=ACT.Square)
        f = tile("f", [P, I])
        nc.gpsimd.tensor_scalar(f[:], sq[:], -0.25, 0.25, ALU.mult, ALU.add)
        bg = tile("bg", [P, I], after=12288)
        for cols in halves:
            nc.scalar.activation(out=bg[:, cols], in_=b[:].indirect(entries(lst2, cols)), func=ACT.Copy)
        factors = tile("factors", [P, 4], after=9216)
        nc.scalar.activation(out=factors[:], in_=cols_ps[:, 0:4], func=ACT.Copy)
        for cols in halves:
            nc.vector.tensor_copy(vg_words[:, cols], v_words[:].bitcast(U32).indirect(entries(lst, cols)))
        for j in range(4):
            cols = slice(j * P, (j + 1) * P)
            nc.tensor.matmul_mx(out=ct_ps[j // 2][:, j % 2, :], lhsT=vg_words[:, cols].bitcast(FP8X4), lhsT_scale=vg_bytes[4:P, cols],
                                rhs=codes["g"][:].bitcast(FP8X4), rhs_scale=planes["g"][:], start=True, stop=True)
        s = tile("s", [P, I], after=0)
        nc.vector.scalar_tensor_tensor(s[:, 0:256], bg[:, 0:256], lam_col, a_ps[0][:, 0:256], ALU.mult, ALU.add)
        nc.vector.scalar_tensor_tensor(s[:, 256:512], bg[:, 256:512], lam_col, a_ps[1][:, 0:256], ALU.mult, ALU.add)
        ct = tile("ct", [P, 4, Q])
        for j in range(2):
            nc.scalar.activation(out=ct[:, j, :], in_=ct_ps[0][:, j, :], func=ACT.Copy, scale=factors[:, j : j + 1])
            nc.tensor.transpose(c_ps[:, j * P : (j + 1) * P], ct[:, j, :], ident[:])
        for j in range(2, 4):
            nc.scalar.activation(out=ct[:, j, :], in_=ct_ps[1][:, j - 2, :], func=ACT.Copy, scale=factors[:, j : j + 1])
            nc.tensor.transpose(c_ps[:, j * P : (j + 1) * P], ct[:, j, :], ident[:])
        neg_max = tile("neg_max", [P, 1])
        nc.vector.tensor_reduce(neg_max[:], s[:], AX.X, ALU.max, negate=True)
        p = tile("p", [P, I])
        z = tile("z", [P, 1])
        nc.scalar.activation(out=p[:], in_=s[:], func=ACT.Exp, bias=neg_max[:], accum_out=z[:])
        xb = tile("xb", [P, I], after=13312)
        nc.vector.tensor_tensor(xb[:], f[:], ta_ps[:], ALU.mult)
        xbg = tile("xbg", [P, I])
        for cols in halves:
            nc.scalar.activation(out=xbg[:, cols], in_=xb[:].indirect(entries(lst2, cols)), func=ACT.Copy)
        w = [tile("w0", [P, HALF], after=12288)]
        nc.vector.tensor_tensor(w[0][:], th[:, halves[0]], ta_ps[:, halves[0]], ALU.mult)
        r = tile("r", [P, 1])
        nc.vector.reciprocal(r[:], z[:])
        pn = tile("pn", [P, I])
        nc.gpsimd.tensor_scalar(pn[:], p[:], r[:], 0.0, ALU.mult, ALU.add)
        prod = tile("prod", [P, I])
        m = tile("m", [P, 1])
        nc.vector.scalar_tensor_tensor(prod[:], c_ps[:], r[:], p[:], ALU.mult, ALU.mult, accum_out=m[:])
        w.append(tile("w1", [P, HALF], after="z"))
        nc.vector.tensor_tensor(w[1][:], th[:, halves[1]], ta_ps[:, halves[1]], ALU.mult)
        d = tile("d", [P, I])
        for cols in halves:
            nc.vector.scalar_tensor_tensor(d[:, cols], c_ps[:, cols], m[:], pn[:, cols], ALU.subtract, ALU.mult)
        e1 = tile("e1", [P, I])
        s1 = tile("s1", [P, I])
        for cols in halves:
            nc.scalar.activation(out=e1[:, cols], in_=d[:, cols], func=ACT.Copy, scale=lam_col)
        for cols in halves:
            nc.scalar.activation(out=s1[:].indirect(entries(lst2, cols)), in_=e1[:, cols], func=ACT.Copy)
        xs = tile("xs", [P, I], after="raw_dq")
        nc.vector.scalar_tensor_tensor(xs[:], xbg[:], lam_col, ta_ps[:], ALU.mult, ALU.add)
        prod2 = tile("prod2", [P, I])
        mu = tile("mu", [P, 1])
        nc.vector.scalar_tensor_tensor(prod2[:], xs[:], r[:], p[:], ALU.mult, ALU.mult, accum_out=mu[:])
        u = tile("u", [P, I])
        k = tile("k", [P, 1])
        nc.vector.scalar_tensor_tensor(u[:], xs[:], mu[:], d[:], ALU.subtract, ALU.mult, accum_out=k[:])
        nx = tile("nx", [P, I])
        xe1_a = tile("xe1_a", [P, I - VECTOR_SHARE])
        for cols in (a_cols, v_cols):
            nc.vector.scalar_tensor_tensor(nx[:, cols], pn[:, cols], k[:], u[:, cols], ALU.mult, ALU.subtract)
        nc.vector.tensor_scalar(xe1_a[:], nx[:, a_cols], lam_col, -1.0, ALU.mult, ALU.mult)
        nc.scalar.activation(out=xs1_a[:].indirect(entries(lst2, a_cols)), in_=xe1_a[:], func=ACT.Copy)
        nc.vector.tensor_tensor(xs1_v[:].indirect(entries(lst2, v_cols)), nx[:, v_cols], neg_lam_wide[:], ALU.mult)
        y0 = tile("y0", [P, I])
        nc.vector.scalar_tensor_tensor(y0[:], nx[:], -GAIN, base_sb[:], ALU.mult, ALU.add)
        t1 = tile("t1", [P, I], after="neg_lam_wide")
        nc.vector.tensor_tensor(t1[:, halves[0]], s1[:, halves[0]], w[0][:], ALU.mult)
        nc.vector.tensor_tensor(t1[:, halves[1]], s1[:, halves[1]], w[1][:], ALU.mult)
        t2 = tile("t2", [P, I])
        for cols in halves:
            nc.vector.tensor_tensor(t2[:, cols], xs1_v[:, cols], t1[:, cols], ALU.subtract)
        t3 = tile("t3", [P, I])
        t4 = tile("t4", [P, I])
        y = tile("y", [P, I])
        for cols in ends:
            nc.vector.tensor_tensor(t3[:, cols], t2[:, cols], xs1_a[:, cols], ALU.add)
        for cols in ends:
            nc.vector.scalar_tensor_tensor(t4[:, cols], t3[:, cols], GAIN, f[:, cols], ALU.mult, ALU.mult)
        for cols in ends:
            nc.vector.tensor_tensor(y[:, cols], t4[:, cols], y0[:, cols], ALU.add)
            nc.sync.dma_start(out=out[:, cols], in_=y[:, cols])
